import numpy as np
import ml_dtypes


def mxq(x, axis, fmt="e4m3"):
    dtype, down = {"e4m3": (ml_dtypes.float8_e4m3fn, 7), "e5m2": (ml_dtypes.float8_e5m2, 14)}[fmt]
    v = np.moveaxis(np.asarray(x, np.float32).astype(ml_dtypes.bfloat16).astype(np.float64), axis, -1)
    blocks = v.reshape(v.shape[:-1] + (-1, 32))
    amax = np.abs(blocks).max(-1, keepdims=True)
    byte = np.maximum(np.where(amax > 0, np.frexp(amax)[1] - 1 + 127, 0) - down, 1)
    scale = np.exp2(byte - 127.0)
    codes = (blocks / scale).astype(np.float32).astype(dtype).astype(np.float64)
    return np.moveaxis((codes * scale).reshape(v.shape), -1, axis)


WIDE = False


def mx_kscale(k):
    if not WIDE:
        return np.ones(k)
    levels = np.array([10, -10, 5, -5, 0])
    if k % 512:
        return np.exp2(np.random.permutation(np.resize(levels, k // 32))).repeat(32)
    a = np.empty((k // 512, 16))
    for p in range(k // 512):
        a[p, :8] = np.random.permutation(np.resize(levels, 8))
        for g in range(8):
            far = levels[np.abs(levels - a[p, g]) >= 10]
            a[p, g + 8] = far[np.random.randint(len(far))]
    return np.exp2(a.ravel()).repeat(32)


def f64(x):
    return np.asarray(x).astype(np.float64)


def striped8(idx):
    return np.concatenate([v.reshape(-1, 16).T for v in idx]).astype(np.uint16)


def unstriped8(offs):
    return np.stack([offs[16 * g:16 * g + 16].T.reshape(-1) for g in range(8)]).astype(np.int64)


E2M1 = np.array([0.0, 0.5, 1.0, 1.5, 2.0, 3.0, 4.0, 6.0, -0.0, -0.5, -1.0, -1.5, -2.0, -3.0, -4.0, -6.0])


def pack_weight(w, fmt):
    k, n = w.shape
    w = f64(np.asarray(w, np.float32).astype(ml_dtypes.bfloat16)).reshape(k // 32, 32, n)
    amax = np.abs(w).max(1)
    if fmt == "e4m3":
        byte = np.frexp(amax)[1] - 1 + 127 - 7
    else:
        mant, ex = np.frexp(amax / 6.0)
        byte = np.where(mant > 0.5, ex, ex - 1) + 127
    byte = np.clip(np.where(amax > 0, byte, 1), 1, 254)
    scaled = (w * np.exp2(127.0 - byte)[:, None, :]).reshape(k, n).astype(np.float32)
    by_word = np.ascontiguousarray(scaled.reshape(k // 512, 128, 4, n).transpose(0, 1, 3, 2))
    if fmt == "e4m3":
        words = by_word.astype(ml_dtypes.float8_e4m3fn).view(np.uint8)
    else:
        c = by_word.astype(ml_dtypes.float4_e2m1fn).view(np.uint8) & 0xF
        words = (c[..., 0::2] | (c[..., 1::2] << 4)).reshape(k // 512, 128, 2 * n)
    return np.ascontiguousarray(words), np.ascontiguousarray(byte.astype(np.uint8).reshape(k // 512, 16, n))


def unpack_weight(words, scales, fmt):
    g, _, n = scales.shape
    words = np.ascontiguousarray(words).reshape(g, 128, n, -1)
    if fmt == "e4m3":
        vals = words.view(ml_dtypes.float8_e4m3fn).astype(np.float64)
    else:
        nib = np.empty((g, 128, n, 4), np.uint8)
        nib[..., 0::2] = words & 0xF
        nib[..., 1::2] = words >> 4
        vals = E2M1[nib]
    vals = vals * np.repeat(np.exp2(scales.astype(np.float64) - 127.0), 8, axis=1)[..., None]
    return vals.transpose(0, 1, 3, 2).reshape(g * 512, n)


K, L, M, T, S = 512, 1536, 128, 2048, 512


def setup_inputs():
    n = np.random.standard_normal
    s1 = mx_kscale(K)[:, None]
    s2 = mx_kscale(L)[:, None]
    p_w4 = pack_weight(n((K, M)) / np.sqrt(K) / s1, "e2m1")
    return {
        "xT": (n((K, T)) * s1).astype(np.float32),
        "w4_words": p_w4[0],
        "w4_scales": p_w4[1],
        "c": (n((L, S)) * s2).astype(np.float32),
        "u": (n((L, M)) / np.sqrt(L) / s2).astype(np.float32),
        "wgt": np.repeat(np.random.uniform(0.5, 2.0, (8, S)), 16, axis=0).astype(np.float32),
        "offs": striped8(np.stack([np.random.permutation(T)[:S] for _ in range(8)])),
    }


def reference(xT, w4_words, w4_scales, c, u, wgt, offs):
    idx = unstriped8(offs)
    group = np.arange(K) % 512 // 64
    xg = f64(wgt)[np.arange(K) // 4 % 128] * f64(xT)[np.arange(K)[:, None], idx[group]]
    xT_ = mxq(xg, 0, "e4m3")
    w4_ = unpack_weight(w4_words, w4_scales, "e2m1")
    c_ = mxq(f64(c), 0, "e4m3")
    u_ = mxq(f64(u), 0, "e4m3")
    y = w4_.T @ xT_ + u_.T @ c_
    return y

@@ -1,0 +1,148 @@
+from contextlib import ExitStack
+
+import concourse.mybir as mybir
+
+FLOPS = 268435456
+
+F32 = mybir.dt.float32
+BF16 = mybir.dt.bfloat16
+I32 = mybir.dt.int32
+U32 = mybir.dt.uint32
+U16 = mybir.dt.uint16
+U8 = mybir.dt.uint8
+E4M3 = mybir.dt.float8_e4m3fn_x4
+E2M1 = mybir.dt.float4_e2m1fn_x4
+MULT = mybir.AluOpType.mult
+
+P = 128
+J = 4
+M = 128
+T = 2048
+S = 512
+DENSE = 3
+GROUP = 128
+PIECE = 256
+
+
+def interleave(copy, dst, src):
+    copy(
+        dst.rearrange("p (c i t) -> p c t i", i=4, t=J),
+        src.rearrange("p t (c i) -> p c t i", i=4),
+    )
+
+
+def tile_list_hmix_none_kernel(tc, xT, w4_words, w4_scales, c, u, wgt, offs, out):
+    nc = tc.nc
+    with ExitStack() as ctx:
+        lists = ctx.enter_context(tc.tile_pool(name="lists", bufs=1))
+        keep = ctx.enter_context(tc.tile_pool(name="keep", bufs=1))
+        psum = ctx.enter_context(tc.psum_pool(name="psum", bufs=1))
+
+        offs_sb = lists.tile([P, S // 16], U16, name="offs_sb")
+        wgt_sb = keep.tile([P, S], F32, name="wgt_sb")
+        w4_sb = keep.tile([P, 2 * M], U8, name="w4_sb", align_bytes=64)
+        w4_sc = keep.tile([P, M], U8, name="w4_sc", align_bytes=64)
+        u_raw = keep.tile([P, DENSE, J * M], F32, name="u_raw")
+        xt = [keep.tile([P, T], F32, name="xt%d" % t) for t in range(J)]
+        splits = [[(0, 512)], [(0, 512)], [(0, 256), (256, 384), (384, 512)]]
+        c_raw = [
+            [keep.tile([P, J, hi - lo], F32, name="c_raw%d_%d" % (a, lo)) for lo, hi in splits[a]]
+            for a in range(DENSE)
+        ]
+
+        nc.vector.memset(w4_sc[:].bitcast(I32), 0)
+
+        x_planes = xT.rearrange("(p j) t -> j p t", j=J)
+        nc.sync.dma_start(offs_sb[:], offs)
+        nc.sync.dma_start(out=wgt_sb[:], in_=wgt)
+        nc.sync.dma_start(out=xt[0][:], in_=x_planes[0])
+        nc.sync.dma_start(out=w4_sb[:].bitcast(I32), in_=w4_words[0].bitcast(I32))
+        for q in range(4):
+            nc.sync.dma_start(
+                out=w4_sc[32 * q : 32 * q + 4, :].bitcast(I32),
+                in_=w4_scales[0, 4 * q : 4 * q + 4, :].bitcast(I32),
+            )
+        nc.sync.dma_start(out=u_raw[:], in_=u.rearrange("(a p j) n -> p a (j n)", p=P, j=J))
+        for t in range(1, J):
+            nc.sync.dma_start(out=xt[t][:], in_=x_planes[t])
+        c_rows = c.rearrange("(a p j) n -> a p j n", p=P, j=J)
+        for a in range(DENSE):
+            for k, (lo, hi) in enumerate(splits[a]):
+                nc.sync.dma_start(out=c_raw[a][k][:], in_=c_rows[a, :, :, lo:hi])
+
+        u_codes = keep.tile([P, DENSE, M], U32, name="u_codes", align_bytes=64)
+        u_scales = keep.tile([P, DENSE, M], U8, name="u_scales", align_bytes=64)
+        u_bf = keep.tile([P, DENSE, M * J], BF16, name="u_bf", align_bytes=64)
+        for a in range(DENSE):
+            interleave(nc.vector.tensor_copy, u_bf[:, a, :], u_raw[:, a, :].rearrange("p (j n) -> p j n", j=J))
+        for a in range(DENSE):
+            nc.vector.quantize_mx(out=u_codes[:, a, :].bitcast(E4M3), scales=u_scales[:, a, :], in_=u_bf[:, a, :])
+
+        halves = S // PIECE
+        picked = [keep.tile([P, J, PIECE], F32, name="picked%d" % h) for h in range(halves)]
+        for t in range(J):
+            for h in range(halves):
+                nc.vector.tensor_tensor(
+                    picked[h][:, t, :],
+                    xt[t][:].indirect(offs_sb[:, h * PIECE // 16 : (h + 1) * PIECE // 16]),
+                    wgt_sb[:, h * PIECE : (h + 1) * PIECE],
+                    MULT,
+                )
+
+        x_codes = keep.tile([P, S], U32, name="x_codes", align_bytes=64)
+        x_scales = keep.tile([P, S], U8, name="x_scales", align_bytes=64)
+        x_bf = [keep.tile([P, PIECE * J], BF16, name="x_bf%d" % h, align_bytes=64) for h in range(halves)]
+        for h in range(halves):
+            interleave(nc.scalar.copy, x_bf[h][:], picked[h][:])
+        for h in range(halves):
+            cols = slice(h * PIECE, (h + 1) * PIECE)
+            nc.vector.quantize_mx(out=x_codes[:, cols].bitcast(E4M3), scales=x_scales[:, cols], in_=x_bf[h][:])
+
+        groups = S // GROUP
+        acc = [psum.tile([M, GROUP], F32, name="acc%d" % g) for g in range(groups)]
+        for g in range(groups):
+            cols = slice(g * GROUP, (g + 1) * GROUP)
+            nc.tensor.matmul_mx(
+                out=acc[g][:],
+                lhsT=w4_sb[:].bitcast(E2M1),
+                lhsT_scale=w4_sc[:],
+                rhs=x_codes[:, cols].bitcast(E4M3),
+                rhs_scale=x_scales[:, cols],
+                start=True,
+                stop=False,
+            )
+
+        c_codes = [keep.tile([P, S], U32, name="c_codes%d" % a, align_bytes=64) for a in range(DENSE)]
+        c_scales = [keep.tile([P, S], U8, name="c_scales%d" % a, align_bytes=64) for a in range(DENSE)]
+        c_bf = [keep.tile([P, S * J], BF16, name="c_bf%d" % a, align_bytes=64) for a in range(DENSE)]
+        res = [keep.tile([M, GROUP], F32, name="res%d" % g) for g in range(groups)]
+        pieces = [
+            (0, 0, 0, 256, nc.vector.tensor_copy),
+            (0, 0, 256, 512, nc.scalar.copy),
+            (1, 0, 0, 256, nc.vector.tensor_copy),
+            (1, 0, 256, 512, nc.scalar.copy),
+            (2, 0, 0, 128, nc.vector.tensor_copy),
+            (2, 0, 128, 256, nc.scalar.copy),
+            (2, 1, 256, 384, nc.scalar.copy),
+            (2, 2, 384, 512, nc.vector.tensor_copy),
+        ]
+        for a, k, lo, hi, copy in pieces:
+            base = splits[a][k][0]
+            interleave(copy, c_bf[a][:, lo * J : hi * J], c_raw[a][k][:, :, lo - base : hi - base])
+            nc.vector.quantize_mx(
+                out=c_codes[a][:, lo:hi].bitcast(E4M3), scales=c_scales[a][:, lo:hi], in_=c_bf[a][:, lo * J : hi * J]
+            )
+            for g in range(lo // GROUP, hi // GROUP):
+                cols = slice(g * GROUP, (g + 1) * GROUP)
+                nc.tensor.matmul_mx(
+                    out=acc[g][:],
+                    lhsT=u_codes[:, a, :].bitcast(E4M3),
+                    lhsT_scale=u_scales[:, a, :],
+                    rhs=c_codes[a][:, cols].bitcast(E4M3),
+                    rhs_scale=c_scales[a][:, cols],
+                    start=False,
+                    stop=(a == DENSE - 1),
+                )
+                if a == DENSE - 1:
+                    nc.scalar.copy(res[g][:], acc[g][:])
+                    nc.sync.dma_start(out=out[:, cols], in_=res[g][:])

@@ -68,7 +68,10 @@ def tile_list_hmix_none_kernel(tc, xT, w4_words, w4_scales, c, u, wgt, offs, out
         c_rows = c.rearrange("(a p j) n -> a p j n", p=P, j=J)
         for a in range(DENSE):
             for k, (lo, hi) in enumerate(splits[a]):
-                nc.sync.dma_start(out=c_raw[a][k][:], in_=c_rows[a, :, :, lo:hi])
+                dst, src = c_raw[a][k][:], c_rows[a, :, :, lo:hi]
+                if hi - lo == S:
+                    dst, src = dst.rearrange("p j n -> p (j n)"), src.rearrange("p j n -> p (j n)")
+                nc.sync.dma_start(out=dst, in_=src)
 
         u_codes = keep.tile([P, DENSE, M], U32, name="u_codes", align_bytes=64)
         u_scales = keep.tile([P, DENSE, M], U8, name="u_scales", align_bytes=64)
@@ -116,22 +119,28 @@ def tile_list_hmix_none_kernel(tc, xT, w4_words, w4_scales, c, u, wgt, offs, out
         c_scales = [keep.tile([P, S], U8, name="c_scales%d" % a, align_bytes=64) for a in range(DENSE)]
         c_bf = [keep.tile([P, S * J], BF16, name="c_bf%d" % a, align_bytes=64) for a in range(DENSE)]
         res = [keep.tile([M, GROUP], F32, name="res%d" % g) for g in range(groups)]
+        vec, sca = nc.vector.tensor_copy, nc.scalar.copy
         pieces = [
-            (0, 0, 0, 256, nc.vector.tensor_copy),
-            (0, 0, 256, 512, nc.scalar.copy),
-            (1, 0, 0, 256, nc.vector.tensor_copy),
-            (1, 0, 256, 512, nc.scalar.copy),
-            (2, 0, 0, 128, nc.vector.tensor_copy),
-            (2, 0, 128, 256, nc.scalar.copy),
-            (2, 1, 256, 384, nc.scalar.copy),
-            (2, 2, 384, 512, nc.vector.tensor_copy),
+            (0, 0, (0, 256), [(0, 256, vec)]),
+            (0, 0, (256, 512), [(256, 512, sca)]),
+            (1, 0, (0, 256), [(0, 256, vec)]),
+            (1, 0, (256, 512), [(256, 512, sca)]),
+            (2, 0, (0, 128), [(0, 128, vec)]),
+            (2, 0, (128, 256), [(128, 256, sca)]),
+            (2, 1, (256, 384), [(256, 384, sca)]),
+            (2, 2, (384, 512), [(384, 448, vec), (448, 512, vec)]),
         ]
-        for a, k, lo, hi, copy in pieces:
+        for a, k, (lo, hi), shares in pieces:
             base = splits[a][k][0]
-            interleave(copy, c_bf[a][:, lo * J : hi * J], c_raw[a][k][:, :, lo - base : hi - base])
-            nc.vector.quantize_mx(
-                out=c_codes[a][:, lo:hi].bitcast(E4M3), scales=c_scales[a][:, lo:hi], in_=c_bf[a][:, lo * J : hi * J]
-            )
+            for s_lo, s_hi, copy in shares:
+                interleave(copy, c_bf[a][:, s_lo * J : s_hi * J], c_raw[a][k][:, :, s_lo - base : s_hi - base])
+            cuts = [(lo, hi)] if len(shares) == 1 else [(s_lo, s_hi) for s_lo, s_hi, copy in shares]
+            for q_lo, q_hi in cuts:
+                nc.vector.quantize_mx(
+                    out=c_codes[a][:, q_lo:q_hi].bitcast(E4M3),
+                    scales=c_scales[a][:, q_lo:q_hi],
+                    in_=c_bf[a][:, q_lo * J : q_hi * J],
+                )
             for g in range(lo // GROUP, hi // GROUP):
                 cols = slice(g * GROUP, (g + 1) * GROUP)
                 nc.tensor.matmul_mx(
@@ -144,5 +153,5 @@ def tile_list_hmix_none_kernel(tc, xT, w4_words, w4_scales, c, u, wgt, offs, out
                     stop=(a == DENSE - 1),
                 )
                 if a == DENSE - 1:
-                    nc.scalar.copy(res[g][:], acc[g][:])
+                    (vec if g == groups - 1 else sca)(res[g][:], acc[g][:])
                     nc.sync.dma_start(out=out[:, cols], in_=res[g][:])

@@ -62,9 +62,10 @@ def tile_list_hmix_none_kernel(tc, xT, w4_words, w4_scales, c, u, wgt, offs, out
                 out=w4_sc[32 * q : 32 * q + 4, :].bitcast(I32),
                 in_=w4_scales[0, 4 * q : 4 * q + 4, :].bitcast(I32),
             )
+        nc.scalar.dma_start(out=xt[1][:], in_=x_planes[1])
         nc.sync.dma_start(out=u_raw[:], in_=u.rearrange("(a p j) n -> p a (j n)", p=P, j=J))
-        for t in range(1, J):
-            nc.sync.dma_start(out=xt[t][:], in_=x_planes[t])
+        nc.sync.dma_start(out=xt[2][:], in_=x_planes[2])
+        nc.scalar.dma_start(out=xt[3][:], in_=x_planes[3])
         c_rows = c.rearrange("(a p j) n -> a p j n", p=P, j=J)
         for a in range(DENSE):
             for k, (lo, hi) in enumerate(splits[a]):

from contextlib import ExitStack

import concourse.mybir as mybir

FLOPS = 268435456

F32 = mybir.dt.float32
BF16 = mybir.dt.bfloat16
I32 = mybir.dt.int32
U32 = mybir.dt.uint32
U16 = mybir.dt.uint16
U8 = mybir.dt.uint8
E4M3 = mybir.dt.float8_e4m3fn_x4
E2M1 = mybir.dt.float4_e2m1fn_x4
MULT = mybir.AluOpType.mult

P = 128
J = 4
M = 128
T = 2048
S = 512
DENSE = 3
GROUP = 128
PIECE = 256


def interleave(copy, dst, src):
    copy(
        dst.rearrange("p (c i t) -> p c t i", i=4, t=J),
        src.rearrange("p t (c i) -> p c t i", i=4),
    )


def tile_list_hmix_none_kernel(tc, xT, w4_words, w4_scales, c, u, wgt, offs, out):
    nc = tc.nc
    with ExitStack() as ctx:
        lists = ctx.enter_context(tc.tile_pool(name="lists", bufs=1))
        keep = ctx.enter_context(tc.tile_pool(name="keep", bufs=1))
        psum = ctx.enter_context(tc.psum_pool(name="psum", bufs=1))

        offs_sb = lists.tile([P, S // 16], U16, name="offs_sb")
        wgt_sb = keep.tile([P, S], F32, name="wgt_sb")
        w4_sb = keep.tile([P, 2 * M], U8, name="w4_sb", align_bytes=64)
        w4_sc = keep.tile([P, M], U8, name="w4_sc", align_bytes=64)
        u_raw = keep.tile([P, DENSE, J * M], F32, name="u_raw")
        xt = [keep.tile([P, T], F32, name="xt%d" % t) for t in range(J)]
        splits = [[(0, 512)], [(0, 512)], [(0, 256), (256, 384), (384, 512)]]
        c_raw = [
            [keep.tile([P, J, hi - lo], F32, name="c_raw%d_%d" % (a, lo)) for lo, hi in splits[a]]
            for a in range(DENSE)
        ]

        nc.vector.memset(w4_sc[:].bitcast(I32), 0)

        x_planes = xT.rearrange("(p j) t -> j p t", j=J)
        nc.sync.dma_start(offs_sb[:], offs)
        nc.sync.dma_start(out=wgt_sb[:], in_=wgt)
        nc.sync.dma_start(out=xt[0][:], in_=x_planes[0])
        nc.sync.dma_start(out=w4_sb[:].bitcast(I32), in_=w4_words[0].bitcast(I32))
        for q in range(4):
            nc.sync.dma_start(
                out=w4_sc[32 * q : 32 * q + 4, :].bitcast(I32),
                in_=w4_scales[0, 4 * q : 4 * q + 4, :].bitcast(I32),
            )
        nc.scalar.dma_start(out=xt[1][:], in_=x_planes[1])
        nc.sync.dma_start(out=u_raw[:], in_=u.rearrange("(a p j) n -> p a (j n)", p=P, j=J))
        nc.sync.dma_start(out=xt[2][:], in_=x_planes[2])
        nc.scalar.dma_start(out=xt[3][:], in_=x_planes[3])
        c_rows = c.rearrange("(a p j) n -> a p j n", p=P, j=J)
        for a in range(DENSE):
            for k, (lo, hi) in enumerate(splits[a]):
                dst, src = c_raw[a][k][:], c_rows[a, :, :, lo:hi]
                if hi - lo == S:
                    dst, src = dst.rearrange("p j n -> p (j n)"), src.rearrange("p j n -> p (j n)")
                nc.sync.dma_start(out=dst, in_=src)

        u_codes = keep.tile([P, DENSE, M], U32, name="u_codes", align_bytes=64)
        u_scales = keep.tile([P, DENSE, M], U8, name="u_scales", align_bytes=64)
        u_bf = keep.tile([P, DENSE, M * J], BF16, name="u_bf", align_bytes=64)
        for a in range(DENSE):
            interleave(nc.vector.tensor_copy, u_bf[:, a, :], u_raw[:, a, :].rearrange("p (j n) -> p j n", j=J))
        for a in range(DENSE):
            nc.vector.quantize_mx(out=u_codes[:, a, :].bitcast(E4M3), scales=u_scales[:, a, :], in_=u_bf[:, a, :])

        halves = S // PIECE
        picked = [keep.tile([P, J, PIECE], F32, name="picked%d" % h) for h in range(halves)]
        for t in range(J):
            for h in range(halves):
                nc.vector.tensor_tensor(
                    picked[h][:, t, :],
                    xt[t][:].indirect(offs_sb[:, h * PIECE // 16 : (h + 1) * PIECE // 16]),
                    wgt_sb[:, h * PIECE : (h + 1) * PIECE],
                    MULT,
                )

        x_codes = keep.tile([P, S], U32, name="x_codes", align_bytes=64)
        x_scales = keep.tile([P, S], U8, name="x_scales", align_bytes=64)
        x_bf = [keep.tile([P, PIECE * J], BF16, name="x_bf%d" % h, align_bytes=64) for h in range(halves)]
        for h in range(halves):
            interleave(nc.scalar.copy, x_bf[h][:], picked[h][:])
        for h in range(halves):
            cols = slice(h * PIECE, (h + 1) * PIECE)
            nc.vector.quantize_mx(out=x_codes[:, cols].bitcast(E4M3), scales=x_scales[:, cols], in_=x_bf[h][:])

        groups = S // GROUP
        acc = [psum.tile([M, GROUP], F32, name="acc%d" % g) for g in range(groups)]
        for g in range(groups):
            cols = slice(g * GROUP, (g + 1) * GROUP)
            nc.tensor.matmul_mx(
                out=acc[g][:],
                lhsT=w4_sb[:].bitcast(E2M1),
                lhsT_scale=w4_sc[:],
                rhs=x_codes[:, cols].bitcast(E4M3),
                rhs_scale=x_scales[:, cols],
                start=True,
                stop=False,
            )

        c_codes = [keep.tile([P, S], U32, name="c_codes%d" % a, align_bytes=64) for a in range(DENSE)]
        c_scales = [keep.tile([P, S], U8, name="c_scales%d" % a, align_bytes=64) for a in range(DENSE)]
        c_bf = [keep.tile([P, S * J], BF16, name="c_bf%d" % a, align_bytes=64) for a in range(DENSE)]
        res = [keep.tile([M, GROUP], F32, name="res%d" % g) for g in range(groups)]
        vec, sca = nc.vector.tensor_copy, nc.scalar.copy
        pieces = [
            (0, 0, (0, 256), [(0, 256, vec)]),
            (0, 0, (256, 512), [(256, 512, sca)]),
            (1, 0, (0, 256), [(0, 256, vec)]),
            (1, 0, (256, 512), [(256, 512, sca)]),
            (2, 0, (0, 128), [(0, 128, vec)]),
            (2, 0, (128, 256), [(128, 256, sca)]),
            (2, 1, (256, 384), [(256, 384, sca)]),
            (2, 2, (384, 512), [(384, 448, vec), (448, 512, vec)]),
        ]
        for a, k, (lo, hi), shares in pieces:
            base = splits[a][k][0]
            for s_lo, s_hi, copy in shares:
                interleave(copy, c_bf[a][:, s_lo * J : s_hi * J], c_raw[a][k][:, :, s_lo - base : s_hi - base])
            cuts = [(lo, hi)] if len(shares) == 1 else [(s_lo, s_hi) for s_lo, s_hi, copy in shares]
            for q_lo, q_hi in cuts:
                nc.vector.quantize_mx(
                    out=c_codes[a][:, q_lo:q_hi].bitcast(E4M3),
                    scales=c_scales[a][:, q_lo:q_hi],
                    in_=c_bf[a][:, q_lo * J : q_hi * J],
                )
            for g in range(lo // GROUP, hi // GROUP):
                cols = slice(g * GROUP, (g + 1) * GROUP)
                nc.tensor.matmul_mx(
                    out=acc[g][:],
                    lhsT=u_codes[:, a, :].bitcast(E4M3),
                    lhsT_scale=u_scales[:, a, :],
                    rhs=c_codes[a][:, cols].bitcast(E4M3),
                    rhs_scale=c_scales[a][:, cols],
                    start=False,
                    stop=(a == DENSE - 1),
                )
                if a == DENSE - 1:
                    (vec if g == groups - 1 else sca)(res[g][:], acc[g][:])
                    nc.sync.dma_start(out=out[:, cols], in_=res[g][:])
